import numpy as np
import ml_dtypes


def mxq(x, axis, fmt="e4m3"):
    dtype, down = {"e4m3": (ml_dtypes.float8_e4m3fn, 7), "e5m2": (ml_dtypes.float8_e5m2, 14)}[fmt]
    v = np.moveaxis(np.asarray(x, np.float32).astype(ml_dtypes.bfloat16).astype(np.float64), axis, -1)
    blocks = v.reshape(v.shape[:-1] + (-1, 32))
    amax = np.abs(blocks).max(-1, keepdims=True)
    byte = np.maximum(np.where(amax > 0, np.frexp(amax)[1] - 1 + 127, 0) - down, 1)
    scale = np.exp2(byte - 127.0)
    codes = (blocks / scale).astype(np.float32).astype(dtype).astype(np.float64)
    return np.moveaxis((codes * scale).reshape(v.shape), -1, axis)


WIDE = False


def mx_kscale(k):
    if not WIDE:
        return np.ones(k)
    levels = np.array([10, -10, 5, -5, 0])
    if k % 512:
        return np.exp2(np.random.permutation(np.resize(levels, k // 32))).repeat(32)
    a = np.empty((k // 512, 16))
    for p in range(k // 512):
        a[p, :8] = np.random.permutation(np.resize(levels, 8))
        for g in range(8):
            far = levels[np.abs(levels - a[p, g]) >= 10]
            a[p, g + 8] = far[np.random.randint(len(far))]
    return np.exp2(a.ravel()).repeat(32)


def f64(x):
    return np.asarray(x).astype(np.float64)


def striped(idx):
    return np.tile(idx.reshape(-1, 16).T, (8, 1)).astype(np.uint16)


def unstriped(offs):
    return offs[:16].T.reshape(-1).astype(np.int64)


def gelu(v):
    return 0.5 * v * (1.0 + np.tanh(np.sqrt(2.0 / np.pi) * (v + 0.044715 * v**3)))


K, T, D, V, H, N = 1024, 512, 4, 256, 512, 256
P = 2 ** 7


def setup_inputs():
    n = np.random.standard_normal
    s = mx_kscale(K)[:, None]
    u = mx_kscale(H)
    return {
        "xT": (n((K, T)) * s).astype(np.float32),
        "w1": (n((K, H)) / np.sqrt(K) / s * u).astype(np.float32),
        "w2": (n((H, N)) / np.sqrt(H) / u[:, None]).astype(np.float32),
        "gate": np.tile(np.random.uniform(0.2, 1.0, (D, 1, V)) / np.sqrt(D), (1, P, 1)).astype(np.float32),
        "pos1": striped(np.random.permutation(T)[:V]),
        "pos2": striped(np.random.permutation(T)[:V]),
        "pos3": striped(np.random.permutation(T)[:V]),
        "pos4": striped(np.random.permutation(T)[:V]),
    }


def reference(xT, w1, w2, gate, pos1, pos2, pos3, pos4):
    h = gelu(mxq(f64(w1), 0, "e4m3").T @ mxq(f64(xT), 0, "e4m3"))
    z = sum(f64(gate)[d, :1] * h[:, unstriped(p)] for d, p in enumerate((pos1, pos2, pos3, pos4)))
    return mxq(f64(w2), 0, "e4m3").T @ mxq(z, 0, "e4m3")

@@ -1,0 +1,205 @@
+from contextlib import ExitStack
+
+import concourse.mybir as mybir
+from concourse.masks import make_identity
+
+K, T, D, V, H, N = 1024, 512, 4, 256, 512, 256
+FLOPS = 2 * K * T * H + 2 * H * N * V
+
+F32 = mybir.dt.float32
+BF16 = mybir.dt.bfloat16
+U32 = mybir.dt.uint32
+U16 = mybir.dt.uint16
+U8 = mybir.dt.uint8
+FP8X4 = mybir.dt.float8_e4m3fn_x4
+MULT = mybir.AluOpType.mult
+GELU = mybir.ActivationFunctionType.Gelu_apprx_tanh
+
+P = 128
+PACK = 4
+PASSES = K // (P * PACK)
+TILES = H // P
+BLOCKS = V // P
+X_CHUNKS = ((0, 0, 512), (1, 0, 384), (1, 384, 128))
+W1_BLOCKS = ((0, 128), (128, 128), (256, 256))
+
+
+def interleave(engine_copy, dst, src):
+    engine_copy(
+        out=dst.rearrange("p (c i) j -> p c j i", i=4),
+        in_=src.rearrange("p j (c i) -> p c j i", i=4),
+    )
+
+
+def quantize(nc, codes, scales, grouped):
+    nc.vector.quantize_mx(
+        out=codes.bitcast(FP8X4), scales=scales, in_=grouped.rearrange("p c j -> p (c j)")
+    )
+
+
+def tile_picked_gcn_mlp_gelu_sub_l_kernel(
+    tc, xT, w1, w2, gate, pos1, pos2, pos3, pos4, out
+):
+    nc = tc.nc
+    with ExitStack() as ctx:
+        keep = ctx.enter_context(tc.tile_pool(name="keep", bufs=1))
+        psum = ctx.enter_context(tc.psum_pool(name="psum", bufs=1))
+
+        w1_raw = [[keep.tile([P, PACK, n], F32, name=f"w1_raw{i}_{c}") for c in range(PASSES)] for i, (i0, n) in enumerate(W1_BLOCKS)]
+        w1_grp = [[keep.tile([P, P, PACK], BF16, align_bytes=64, name=f"w1_grp{t}_{c}") for c in range(PASSES)] for t in range(TILES)]
+        w1_codes = [[keep.tile([P, P], U32, align_bytes=64, name=f"w1_codes{t}_{c}") for c in range(PASSES)] for t in range(TILES)]
+        w1_scales = [[keep.tile([P, P], U8, align_bytes=64, name=f"w1_scales{t}_{c}") for c in range(PASSES)] for t in range(TILES)]
+        x_raw = [keep.tile([P, PACK, n], F32, name=f"x_raw{i}") for i, (c, n0, n) in enumerate(X_CHUNKS)]
+        x_grp = [keep.tile([P, n, PACK], BF16, align_bytes=64, name=f"x_grp{i}") for i, (c, n0, n) in enumerate(X_CHUNKS)]
+        x_codes = keep.tile([P, PASSES, T], U32, align_bytes=64, name="x_codes")
+        x_scales = keep.tile([P, PASSES, T], U8, align_bytes=64, name="x_scales")
+        w2_raw = keep.tile([P, PACK, N], F32, name="w2_raw")
+        w2_grp = keep.tile([P, N, PACK], BF16, align_bytes=64, name="w2_grp")
+        w2_codes = keep.tile([P, N], U32, align_bytes=64, name="w2_codes")
+        w2_scales = keep.tile([P, N], U8, align_bytes=64, name="w2_scales")
+        gate_sb = [keep.tile([P, 2, V], F32, name=f"gate{d}") for d in range(2)]
+        lists = [keep.tile([P, V // 16], U16, name=f"list{d}") for d in range(D)]
+        ident = keep.tile([P, P], F32, name="ident")
+        warm = keep.tile([P, 1], F32, name="warm")
+
+        xr = xT.rearrange("(c p j) t -> c p j t", p=P, j=PACK)
+        w1r = w1.rearrange("(c p j) i -> c p j i", p=P, j=PACK)
+
+        def load_w1(i):
+            i0, n = W1_BLOCKS[i]
+            for c in range(PASSES):
+                nc.sync.dma_start(out=w1_raw[i][c][:], in_=w1r[c, :, :, i0 : i0 + n])
+
+        def load_x(i):
+            c, n0, n = X_CHUNKS[i]
+            nc.sync.dma_start(out=x_raw[i][:], in_=xr[c, :, :, n0 : n0 + n])
+
+        load_w1(0)
+        load_x(0)
+        load_x(1)
+        for d, pos in enumerate((pos1, pos2, pos3, pos4)):
+            nc.sync.dma_start(lists[d][:], pos)
+        load_x(2)
+        nc.sync.dma_start(out=gate_sb[0][:], in_=gate[0:2].rearrange("d p v -> p d v"))
+        load_w1(1)
+        nc.sync.dma_start(out=gate_sb[1][:], in_=gate[2:4].rearrange("d p v -> p d v"))
+        load_w1(2)
+        nc.sync.dma_start(out=w2_raw[:], in_=w2.rearrange("(p j) m -> p j m", j=PACK))
+
+        nc.gpsimd.memset(warm[:], 0.0)
+        nc.scalar.activation(warm[:], warm[:], GELU)
+        make_identity(nc, ident[:])
+
+        def prepare_w1(t, copies):
+            i = min(t, 2)
+            i0 = t * P - W1_BLOCKS[i][0]
+            for c in range(PASSES):
+                interleave(copies[c], w1_grp[t][c][:], w1_raw[i][c][:, :, i0 : i0 + P])
+            for c in range(PASSES):
+                quantize(nc, w1_codes[t][c][:], w1_scales[t][c][:], w1_grp[t][c][:])
+
+        h_sb = [keep.tile([P, T], F32, name=f"h{t}") for t in range(TILES)]
+
+        def project(t, spans):
+            bank = psum.tile([P, T], F32, name=f"h_bank{t % 3}")
+            for n0, n in spans:
+                for c in range(PASSES):
+                    nc.tensor.matmul_mx(
+                        out=bank[:, n0 : n0 + n],
+                        lhsT=w1_codes[t][c][:].bitcast(FP8X4),
+                        lhsT_scale=w1_scales[t][c][:],
+                        rhs=x_codes[:, c, n0 : n0 + n].bitcast(FP8X4),
+                        rhs_scale=x_scales[:, c, n0 : n0 + n],
+                        start=(c == 0),
+                        stop=(c == PASSES - 1),
+                    )
+            for n0, n in spans:
+                nc.scalar.activation(h_sb[t][:, n0 : n0 + n], bank[:, n0 : n0 + n], GELU)
+
+        def quantize_x(i, a, n):
+            c, n0, m = X_CHUNKS[i]
+            quantize(nc, x_codes[:, c, n0 + a : n0 + a + n], x_scales[:, c, n0 + a : n0 + a + n], x_grp[i][:, a : a + n, :])
+
+        prepare_w1(0, (nc.vector.tensor_copy, nc.scalar.copy))
+        interleave(nc.vector.tensor_copy, x_grp[0][:, 0:256, :], x_raw[0][:, :, 0:256])
+        interleave(nc.scalar.copy, x_grp[0][:, 256:512, :], x_raw[0][:, :, 256:512])
+        quantize_x(0, 0, 256)
+        quantize_x(0, 256, 256)
+        interleave(nc.vector.tensor_copy, x_grp[1][:, 0:256, :], x_raw[1][:, :, 0:256])
+        interleave(nc.vector.tensor_copy, x_grp[1][:, 256:384, :], x_raw[1][:, :, 256:384])
+        interleave(nc.scalar.copy, x_grp[2][:], x_raw[2][:])
+        quantize_x(1, 0, 256)
+        quantize_x(1, 256, 128)
+        quantize_x(2, 0, 128)
+        project(0, ((0, 256), (256, 128), (384, 128)))
+
+        z_bank = [psum.tile([P, H], F32, name=f"z_bank{b}") for b in range(BLOCKS)]
+        z_rows = [keep.tile([P, PACK, P], F32, name=f"z_rows{b}") for b in range(BLOCKS)]
+
+        def gather(t, d, v0, n):
+            g = keep.tile([P, n], F32, name=f"g{t}_{d}_{v0}")
+            nc.vector.tensor_tensor(
+                g[:], h_sb[t][:].indirect(lists[d][:, v0 // 16 : (v0 + n) // 16]), gate_sb[d // 2][:, d % 2, v0 : v0 + n], MULT
+            )
+            return g
+
+        def add_up(t, b, parts):
+            for d in range(D):
+                nc.tensor.matmul(
+                    z_bank[b][:, t * P : (t + 1) * P],
+                    lhsT=parts[d],
+                    rhs=ident[:],
+                    is_transpose=True,
+                    start=(d == 0),
+                    stop=(d == D - 1),
+                )
+
+        def sort_rows(b, c0, c1):
+            nc.scalar.copy(
+                z_rows[b][:, :, c0 // PACK : c1 // PACK],
+                z_bank[b][:, c0:c1].rearrange("v (m s) -> v s m", s=PACK),
+            )
+
+        for t in range(TILES - 1):
+            split = 3 - t
+            parts = [gather(t, d, 0, V) for d in range(split)]
+            prepare_w1(t + 1, (nc.scalar.copy, nc.scalar.copy))
+            project(t + 1, ((0, 512),))
+            parts += [gather(t, d, 0, V) for d in range(split, D)]
+            for b in range(BLOCKS):
+                add_up(t, b, [g[:, b * P : (b + 1) * P] for g in parts])
+        interleave(nc.scalar.copy, w2_grp[:], w2_raw[:])
+        outr = out.rearrange("(a p) v -> p a v", p=P)
+        t = TILES - 1
+        for b in range(BLOCKS):
+            sort_rows(b, 0, t * P)
+            parts = [gather(t, d, b * P, P) for d in range(D)]
+            if b == 0:
+                quantize(nc, w2_codes[:], w2_scales[:], w2_grp[:])
+            add_up(t, b, [g[:] for g in parts])
+            sort_rows(b, t * P, H)
+            back = psum.tile([P, PACK, P], F32, name="back")
+            for s in range(PACK):
+                nc.tensor.transpose(back[:, s, :], z_rows[b][:, s, :], ident[:])
+            z_grp = keep.tile([P, P, PACK], BF16, align_bytes=64, name=f"z_grp{b}")
+            nc.scalar.copy(z_grp[:], back[:].rearrange("p s v -> p v s"))
+            z_codes = keep.tile([P, P], U32, align_bytes=64, name=f"z_codes{b}")
+            z_scales = keep.tile([P, P], U8, align_bytes=64, name=f"z_scales{b}")
+            quantize(nc, z_codes[:], z_scales[:], z_grp[:])
+            for a in range(N // P):
+                o_bank = psum.tile([P, P], F32, name=f"o_bank{a}")
+                o_sb = keep.tile([P, P], F32, name=f"o_sb{b}_{a}")
+                nc.tensor.matmul_mx(
+                    out=o_bank[:],
+                    lhsT=w2_codes[:, a * P : (a + 1) * P].bitcast(FP8X4),
+                    lhsT_scale=w2_scales[:, a * P : (a + 1) * P],
+                    rhs=z_codes[:].bitcast(FP8X4),
+                    rhs_scale=z_scales[:],
+                    start=True,
+                    stop=True,
+                )
+                if a == 0 and b == 1:
+                    nc.vector.tensor_copy(o_sb[:], o_bank[:])
+                else:
+                    nc.scalar.copy(o_sb[:], o_bank[:])
+                nc.sync.dma_start(out=outr[:, a, b * P : (b + 1) * P], in_=o_sb[:])

@@ -46,9 +46,9 @@ def tile_picked_gcn_mlp_gelu_sub_l_kernel(
         psum = ctx.enter_context(tc.psum_pool(name="psum", bufs=1))
 
         w1_raw = [[keep.tile([P, PACK, n], F32, name=f"w1_raw{i}_{c}") for c in range(PASSES)] for i, (i0, n) in enumerate(W1_BLOCKS)]
-        w1_grp = [[keep.tile([P, P, PACK], BF16, align_bytes=64, name=f"w1_grp{t}_{c}") for c in range(PASSES)] for t in range(TILES)]
-        w1_codes = [[keep.tile([P, P], U32, align_bytes=64, name=f"w1_codes{t}_{c}") for c in range(PASSES)] for t in range(TILES)]
-        w1_scales = [[keep.tile([P, P], U8, align_bytes=64, name=f"w1_scales{t}_{c}") for c in range(PASSES)] for t in range(TILES)]
+        w1_grp = [keep.tile([P, PASSES, P, PACK], BF16, align_bytes=64, name=f"w1_grp{t}") for t in range(TILES)]
+        w1_codes = [keep.tile([P, PASSES, P], U32, align_bytes=64, name=f"w1_codes{t}") for t in range(TILES)]
+        w1_scales = [keep.tile([P, PASSES, P], U8, align_bytes=64, name=f"w1_scales{t}") for t in range(TILES)]
         x_raw = [keep.tile([P, PACK, n], F32, name=f"x_raw{i}") for i, (c, n0, n) in enumerate(X_CHUNKS)]
         x_grp = [keep.tile([P, n, PACK], BF16, align_bytes=64, name=f"x_grp{i}") for i, (c, n0, n) in enumerate(X_CHUNKS)]
         x_codes = keep.tile([P, PASSES, T], U32, align_bytes=64, name="x_codes")
@@ -80,8 +80,8 @@ def tile_picked_gcn_mlp_gelu_sub_l_kernel(
         for d, pos in enumerate((pos1, pos2, pos3, pos4)):
             nc.sync.dma_start(lists[d][:], pos)
         load_x(2)
-        nc.sync.dma_start(out=gate_sb[0][:], in_=gate[0:2].rearrange("d p v -> p d v"))
         load_w1(1)
+        nc.sync.dma_start(out=gate_sb[0][:], in_=gate[0:2].rearrange("d p v -> p d v"))
         nc.sync.dma_start(out=gate_sb[1][:], in_=gate[2:4].rearrange("d p v -> p d v"))
         load_w1(2)
         nc.sync.dma_start(out=w2_raw[:], in_=w2.rearrange("(p j) m -> p j m", j=PACK))
@@ -90,13 +90,17 @@ def tile_picked_gcn_mlp_gelu_sub_l_kernel(
         nc.scalar.activation(warm[:], warm[:], GELU)
         make_identity(nc, ident[:])
 
-        def prepare_w1(t, copies):
+        def regroup_w1(engine_copy, t, c):
             i = min(t, 2)
             i0 = t * P - W1_BLOCKS[i][0]
-            for c in range(PASSES):
-                interleave(copies[c], w1_grp[t][c][:], w1_raw[i][c][:, :, i0 : i0 + P])
-            for c in range(PASSES):
-                quantize(nc, w1_codes[t][c][:], w1_scales[t][c][:], w1_grp[t][c][:])
+            interleave(engine_copy, w1_grp[t][:, c], w1_raw[i][c][:, :, i0 : i0 + P])
+
+        def quantize_w1(t):
+            nc.vector.quantize_mx(
+                out=w1_codes[t][:].rearrange("p c n -> p (c n)").bitcast(FP8X4),
+                scales=w1_scales[t][:].rearrange("p c n -> p (c n)"),
+                in_=w1_grp[t][:].rearrange("p c n j -> p (c n j)"),
+            )
 
         h_sb = [keep.tile([P, T], F32, name=f"h{t}") for t in range(TILES)]
 
@@ -106,8 +110,8 @@ def tile_picked_gcn_mlp_gelu_sub_l_kernel(
                 for c in range(PASSES):
                     nc.tensor.matmul_mx(
                         out=bank[:, n0 : n0 + n],
-                        lhsT=w1_codes[t][c][:].bitcast(FP8X4),
-                        lhsT_scale=w1_scales[t][c][:],
+                        lhsT=w1_codes[t][:, c, :].bitcast(FP8X4),
+                        lhsT_scale=w1_scales[t][:, c, :],
                         rhs=x_codes[:, c, n0 : n0 + n].bitcast(FP8X4),
                         rhs_scale=x_scales[:, c, n0 : n0 + n],
                         start=(c == 0),
@@ -120,18 +124,24 @@ def tile_picked_gcn_mlp_gelu_sub_l_kernel(
             c, n0, m = X_CHUNKS[i]
             quantize(nc, x_codes[:, c, n0 + a : n0 + a + n], x_scales[:, c, n0 + a : n0 + a + n], x_grp[i][:, a : a + n, :])
 
-        prepare_w1(0, (nc.vector.tensor_copy, nc.scalar.copy))
+        regroup_w1(nc.vector.tensor_copy, 0, 0)
+        regroup_w1(nc.scalar.copy, 0, 1)
+        quantize_w1(0)
         interleave(nc.vector.tensor_copy, x_grp[0][:, 0:256, :], x_raw[0][:, :, 0:256])
         interleave(nc.scalar.copy, x_grp[0][:, 256:512, :], x_raw[0][:, :, 256:512])
         quantize_x(0, 0, 256)
         quantize_x(0, 256, 256)
         interleave(nc.vector.tensor_copy, x_grp[1][:, 0:256, :], x_raw[1][:, :, 0:256])
-        interleave(nc.vector.tensor_copy, x_grp[1][:, 256:384, :], x_raw[1][:, :, 256:384])
-        interleave(nc.scalar.copy, x_grp[2][:], x_raw[2][:])
+        interleave(nc.scalar.copy, x_grp[1][:, 256:384, :], x_raw[1][:, :, 256:384])
         quantize_x(1, 0, 256)
+        interleave(nc.vector.tensor_copy, x_grp[2][:], x_raw[2][:])
         quantize_x(1, 256, 128)
         quantize_x(2, 0, 128)
+        regroup_w1(nc.vector.tensor_copy, 1, 0)
+        regroup_w1(nc.vector.tensor_copy, 1, 1)
+        quantize_w1(1)
         project(0, ((0, 256), (256, 128), (384, 128)))
+        project(1, ((0, 512),))
 
         z_bank = [psum.tile([P, H], F32, name=f"z_bank{b}") for b in range(BLOCKS)]
         z_rows = [keep.tile([P, PACK, P], F32, name=f"z_rows{b}") for b in range(BLOCKS)]
@@ -142,6 +152,10 @@ def tile_picked_gcn_mlp_gelu_sub_l_kernel(
                 g[:], h_sb[t][:].indirect(lists[d][:, v0 // 16 : (v0 + n) // 16]), gate_sb[d // 2][:, d % 2, v0 : v0 + n], MULT
             )
             return g
+
+        def add_tile(t, parts):
+            for b in range(BLOCKS):
+                add_up(t, b, [g[:, b * P : (b + 1) * P] for g in parts])
 
         def add_up(t, b, parts):
             for d in range(D):
@@ -154,52 +168,80 @@ def tile_picked_gcn_mlp_gelu_sub_l_kernel(
                     stop=(d == D - 1),
                 )
 
-        def sort_rows(b, c0, c1):
-            nc.scalar.copy(
+        def sort_rows(copy, b, c0, c1):
+            copy(
                 z_rows[b][:, :, c0 // PACK : c1 // PACK],
                 z_bank[b][:, c0:c1].rearrange("v (m s) -> v s m", s=PACK),
             )
 
-        for t in range(TILES - 1):
-            split = 3 - t
-            parts = [gather(t, d, 0, V) for d in range(split)]
-            prepare_w1(t + 1, (nc.scalar.copy, nc.scalar.copy))
-            project(t + 1, ((0, 512),))
-            parts += [gather(t, d, 0, V) for d in range(split, D)]
+        def add_tile(t, parts):
             for b in range(BLOCKS):
                 add_up(t, b, [g[:, b * P : (b + 1) * P] for g in parts])
+
+        for c in range(PASSES):
+            regroup_w1(nc.scalar.copy, 2, c)
+        parts = [gather(0, d, 0, V) for d in range(D)]
+        add_tile(0, parts)
+
+        parts = [gather(1, 0, 0, V)]
+        quantize_w1(2)
+        project(2, ((0, 512),))
+        for c in range(PASSES):
+            regroup_w1(nc.scalar.copy, 3, c)
+        parts += [gather(1, d, 0, V) for d in (1, 2)]
+        quantize_w1(3)
+        project(3, ((0, 512),))
+        parts += [gather(1, 3, 0, V)]
+        add_tile(1, parts)
+
         interleave(nc.scalar.copy, w2_grp[:], w2_raw[:])
-        outr = out.rearrange("(a p) v -> p a v", p=P)
-        t = TILES - 1
+        parts = [gather(2, d, 0, V) for d in (0, 1, 2)]
+        quantize(nc, w2_codes[:], w2_scales[:], w2_grp[:])
+        parts += [gather(2, 3, 0, V)]
+        add_tile(2, parts)
         for b in range(BLOCKS):
-            sort_rows(b, 0, t * P)
-            parts = [gather(t, d, b * P, P) for d in range(D)]
-            if b == 0:
-                quantize(nc, w2_codes[:], w2_scales[:], w2_grp[:])
-            add_up(t, b, [g[:] for g in parts])
-            sort_rows(b, t * P, H)
-            back = psum.tile([P, PACK, P], F32, name="back")
+            sort_rows(nc.scalar.copy, b, 0, 3 * P)
+
+        parts = [gather(3, d, 0, V) for d in (0, 1, 2)]
+        last = [gather(3, 3, b * P, P) for b in range(BLOCKS)]
+        empty = (nc.scalar.copy, nc.vector.tensor_copy)
+        back = [psum.tile([P, PACK, P], F32, name=f"back{b}") for b in range(BLOCKS)]
+        z_grp = [keep.tile([P, P, PACK], BF16, align_bytes=64, name=f"z_grp{b}") for b in range(BLOCKS)]
+        z_codes = [keep.tile([P, P], U32, align_bytes=64, name=f"z_codes{b}") for b in range(BLOCKS)]
+        z_scales = [keep.tile([P, P], U8, align_bytes=64, name=f"z_scales{b}") for b in range(BLOCKS)]
+        for b in range(BLOCKS):
+            add_up(3, b, [g[:, b * P : (b + 1) * P] for g in parts] + [last[b][:]])
+        for b in range(BLOCKS):
+            sort_rows(empty[b], b, 3 * P, H)
+        for b in range(BLOCKS):
             for s in range(PACK):
-                nc.tensor.transpose(back[:, s, :], z_rows[b][:, s, :], ident[:])
-            z_grp = keep.tile([P, P, PACK], BF16, align_bytes=64, name=f"z_grp{b}")
-            nc.scalar.copy(z_grp[:], back[:].rearrange("p s v -> p v s"))
-            z_codes = keep.tile([P, P], U32, align_bytes=64, name=f"z_codes{b}")
-            z_scales = keep.tile([P, P], U8, align_bytes=64, name=f"z_scales{b}")
-            quantize(nc, z_codes[:], z_scales[:], z_grp[:])
-            for a in range(N // P):
-                o_bank = psum.tile([P, P], F32, name=f"o_bank{a}")
-                o_sb = keep.tile([P, P], F32, name=f"o_sb{b}_{a}")
-                nc.tensor.matmul_mx(
-                    out=o_bank[:],
-                    lhsT=w2_codes[:, a * P : (a + 1) * P].bitcast(FP8X4),
-                    lhsT_scale=w2_scales[:, a * P : (a + 1) * P],
-                    rhs=z_codes[:].bitcast(FP8X4),
-                    rhs_scale=z_scales[:],
-                    start=True,
-                    stop=True,
-                )
-                if a == 0 and b == 1:
-                    nc.vector.tensor_copy(o_sb[:], o_bank[:])
-                else:
-                    nc.scalar.copy(o_sb[:], o_bank[:])
-                nc.sync.dma_start(out=outr[:, a, b * P : (b + 1) * P], in_=o_sb[:])
+                nc.tensor.transpose(back[b][:, s, :], z_rows[b][:, s, :], ident[:])
+        for b in range(BLOCKS):
+            empty[b](z_grp[b][:], back[b][:].rearrange("p s v -> p v s"))
+        for b in range(BLOCKS):
+            quantize(nc, z_codes[b][:], z_scales[b][:], z_grp[b][:])
+        outr = out.rearrange("(a p) v -> p a v", p=P)
+
+        def second(bank, b, a):
+            nc.tensor.matmul_mx(
+                out=bank,
+                lhsT=w2_codes[:, a * P : (a + 1) * P].bitcast(FP8X4),
+                lhsT_scale=w2_scales[:, a * P : (a + 1) * P],
+                rhs=z_codes[b][:].bitcast(FP8X4),
+                rhs_scale=z_scales[b][:],
+                start=True,
+                stop=True,
+            )
+
+        o_bank0 = psum.tile([P, T], F32, name="h_bank1")
+        o_sb0 = keep.tile([P, 2, P], F32, name="o_sb0")
+        for a in range(2):
+            second(o_bank0[:, a * P : (a + 1) * P], 0, a)
+        nc.scalar.copy(o_sb0[:], o_bank0[:, 0:256].rearrange("p (a v) -> p a v", a=2))
+        nc.sync.dma_start(out=outr[:, :, 0:P], in_=o_sb0[:])
+        for a, copy, store in ((0, nc.vector.tensor_copy, nc.sync.dma_start), (1, nc.scalar.copy, nc.scalar.dma_start)):
+            o_bank1 = psum.tile([P, T], F32, name=("h_bank2", "o_bank")[a])
+            o_sb1 = keep.tile([P, P], F32, name=f"o_sb1_{a}")
+            second(o_bank1[:, 0:P], 1, a)
+            copy(o_sb1[:], o_bank1[:, 0:P])
+            store(out=outr[:, a, P:V], in_=o_sb1[:])

@@ -46,11 +46,14 @@ def tile_picked_gcn_mlp_gelu_sub_l_kernel(
         psum = ctx.enter_context(tc.psum_pool(name="psum", bufs=1))
 
         w1_raw = [[keep.tile([P, PACK, n], F32, name=f"w1_raw{i}_{c}") for c in range(PASSES)] for i, (i0, n) in enumerate(W1_BLOCKS)]
-        w1_grp = [keep.tile([P, PASSES, P, PACK], BF16, align_bytes=64, name=f"w1_grp{t}") for t in range(TILES)]
         w1_codes = [keep.tile([P, PASSES, P], U32, align_bytes=64, name=f"w1_codes{t}") for t in range(TILES)]
         w1_scales = [keep.tile([P, PASSES, P], U8, align_bytes=64, name=f"w1_scales{t}") for t in range(TILES)]
         x_raw = [keep.tile([P, PACK, n], F32, name=f"x_raw{i}") for i, (c, n0, n) in enumerate(X_CHUNKS)]
-        x_grp = [keep.tile([P, n, PACK], BF16, align_bytes=64, name=f"x_grp{i}") for i, (c, n0, n) in enumerate(X_CHUNKS)]
+        x_grp = [
+            keep.tile([P, n, PACK], BF16, align_bytes=64, name=f"x_grp{i}", tag=("xg0", "xg1", "turn")[i])
+            for i, (c, n0, n) in enumerate(X_CHUNKS)
+        ]
+        w1_grp = {}
         x_codes = keep.tile([P, PASSES, T], U32, align_bytes=64, name="x_codes")
         x_scales = keep.tile([P, PASSES, T], U8, align_bytes=64, name="x_scales")
         w2_raw = keep.tile([P, PACK, N], F32, name="w2_raw")
@@ -74,11 +77,14 @@ def tile_picked_gcn_mlp_gelu_sub_l_kernel(
             c, n0, n = X_CHUNKS[i]
             nc.sync.dma_start(out=x_raw[i][:], in_=xr[c, :, :, n0 : n0 + n])
 
+        def load_list(d):
+            nc.sync.dma_start(lists[d][:], (pos1, pos2, pos3, pos4)[d])
+
         load_w1(0)
         load_x(0)
         load_x(1)
-        for d, pos in enumerate((pos1, pos2, pos3, pos4)):
-            nc.sync.dma_start(lists[d][:], pos)
+        for d in range(D):
+            load_list(d)
         load_x(2)
         load_w1(1)
         nc.sync.dma_start(out=gate_sb[0][:], in_=gate[0:2].rearrange("d p v -> p d v"))
@@ -91,9 +97,17 @@ def tile_picked_gcn_mlp_gelu_sub_l_kernel(
         make_identity(nc, ident[:])
 
         def regroup_w1(engine_copy, t, c):
-            i = min(t, 2)
-            i0 = t * P - W1_BLOCKS[i][0]
-            interleave(engine_copy, w1_grp[t][:, c], w1_raw[i][c][:, :, i0 : i0 + P])
+            if c == 0:
+                w1_grp[t] = keep.tile(
+                    [P, PASSES, P, PACK], BF16, align_bytes=64, name=f"w1_grp{t}", tag=("wg0", "turn", "turn", "wg3")[t]
+                )
+            if t < 2:
+                interleave(engine_copy, w1_grp[t][:, c], w1_raw[t][c][:])
+            else:
+                engine_copy(
+                    out=w1_grp[t][:, c].rearrange("p (m r) j -> p m j r", r=2),
+                    in_=w1_raw[2][c][:].rearrange("p j (m h r) -> p h m j r", h=2, r=2)[:, t - 2],
+                )
 
         def quantize_w1(t):
             nc.vector.quantize_mx(
@@ -168,15 +182,14 @@ def tile_picked_gcn_mlp_gelu_sub_l_kernel(
                     stop=(d == D - 1),
                 )
 
-        def sort_rows(copy, b, c0, c1):
-            copy(
-                z_rows[b][:, :, c0 // PACK : c1 // PACK],
-                z_bank[b][:, c0:c1].rearrange("v (m s) -> v s m", s=PACK),
-            )
-
-        def add_tile(t, parts):
-            for b in range(BLOCKS):
-                add_up(t, b, [g[:, b * P : (b + 1) * P] for g in parts])
+        def sort_rows(copy, b, t):
+            if t < 2:
+                rows = z_rows[b][:, :, t * 32 : (t + 1) * 32]
+                cols = z_bank[b][:, t * P : (t + 1) * P].rearrange("v (m s) -> v s m", s=PACK)
+            else:
+                rows = z_rows[b][:, 2 * t - 4 : 2 * t - 2, 64:128]
+                cols = z_bank[b][:, t * P : (t + 1) * P].rearrange("v (m r) -> v r m", r=2)
+            copy(rows, cols)
 
         for c in range(PASSES):
             regroup_w1(nc.scalar.copy, 2, c)
@@ -195,29 +208,36 @@ def tile_picked_gcn_mlp_gelu_sub_l_kernel(
         add_tile(1, parts)
 
         interleave(nc.scalar.copy, w2_grp[:], w2_raw[:])
-        parts = [gather(2, d, 0, V) for d in (0, 1, 2)]
-        quantize(nc, w2_codes[:], w2_scales[:], w2_grp[:])
-        parts += [gather(2, 3, 0, V)]
+        parts = [gather(2, d, 0, V) for d in range(D)]
         add_tile(2, parts)
-        for b in range(BLOCKS):
-            sort_rows(nc.scalar.copy, b, 0, 3 * P)
-
-        parts = [gather(3, d, 0, V) for d in (0, 1, 2)]
-        last = [gather(3, 3, b * P, P) for b in range(BLOCKS)]
-        empty = (nc.scalar.copy, nc.vector.tensor_copy)
-        back = [psum.tile([P, PACK, P], F32, name=f"back{b}") for b in range(BLOCKS)]
         z_grp = [keep.tile([P, P, PACK], BF16, align_bytes=64, name=f"z_grp{b}") for b in range(BLOCKS)]
         z_codes = [keep.tile([P, P], U32, align_bytes=64, name=f"z_codes{b}") for b in range(BLOCKS)]
         z_scales = [keep.tile([P, P], U8, align_bytes=64, name=f"z_scales{b}") for b in range(BLOCKS)]
+        empty = (nc.scalar.copy, nc.vector.tensor_copy)
+
+        def turn_back(b, u):
+            back = psum.tile([P, 2, P], F32, name=f"back{b}")
+            for r in range(2):
+                nc.tensor.transpose(back[:, r, :], z_rows[b][:, 2 * u + r, :], ident[:])
+            return back
+
+        def round_pair(copy, b, u, back):
+            copy(z_grp[b][:, :, 2 * u : 2 * u + 2], back[:].rearrange("p r v -> p v r"))
+
+        for b in range(BLOCKS):
+            for t in range(3):
+                sort_rows(nc.scalar.copy, b, t)
+            round_pair(nc.scalar.copy, b, 0, turn_back(b, 0))
+        parts = [gather(3, d, 0, V) for d in (0, 1, 2)]
+        last = [gather(3, 3, b * P, P) for b in range(BLOCKS)]
+        quantize(nc, w2_codes[:], w2_scales[:], w2_grp[:])
         for b in range(BLOCKS):
             add_up(3, b, [g[:, b * P : (b + 1) * P] for g in parts] + [last[b][:]])
         for b in range(BLOCKS):
-            sort_rows(empty[b], b, 3 * P, H)
+            sort_rows(empty[b], b, 3)
+        back = [turn_back(b, 1) for b in range(BLOCKS)]
         for b in range(BLOCKS):
-            for s in range(PACK):
-                nc.tensor.transpose(back[b][:, s, :], z_rows[b][:, s, :], ident[:])
-        for b in range(BLOCKS):
-            empty[b](z_grp[b][:], back[b][:].rearrange("p s v -> p v s"))
+            round_pair(empty[b], b, 1, back[b])
         for b in range(BLOCKS):
             quantize(nc, z_codes[b][:], z_scales[b][:], z_grp[b][:])
         outr = out.rearrange("(a p) v -> p a v", p=P)

@@ -13,6 +13,7 @@ U16 = mybir.dt.uint16
 U8 = mybir.dt.uint8
 FP8X4 = mybir.dt.float8_e4m3fn_x4
 MULT = mybir.AluOpType.mult
+ADD = mybir.AluOpType.add
 GELU = mybir.ActivationFunctionType.Gelu_apprx_tanh
 
 P = 128
@@ -20,8 +21,8 @@ PACK = 4
 PASSES = K // (P * PACK)
 TILES = H // P
 BLOCKS = V // P
-X_CHUNKS = ((0, 0, 512), (1, 0, 384), (1, 384, 128))
-W1_BLOCKS = ((0, 128), (128, 128), (256, 256))
+LANES = PACK - 1
+W1_GROUPS = ((0, 43), (43, 86), (85, 128))
 
 
 def interleave(engine_copy, dst, src):
@@ -45,19 +46,22 @@ def tile_picked_gcn_mlp_gelu_sub_l_kernel(
         keep = ctx.enter_context(tc.tile_pool(name="keep", bufs=1))
         psum = ctx.enter_context(tc.psum_pool(name="psum", bufs=1))
 
-        w1_raw = [[keep.tile([P, PACK, n], F32, name=f"w1_raw{i}_{c}") for c in range(PASSES)] for i, (i0, n) in enumerate(W1_BLOCKS)]
-        w1_codes = [keep.tile([P, PASSES, P], U32, align_bytes=64, name=f"w1_codes{t}") for t in range(TILES)]
-        w1_scales = [keep.tile([P, PASSES, P], U8, align_bytes=64, name=f"w1_scales{t}") for t in range(TILES)]
-        x_raw = [keep.tile([P, PACK, n], F32, name=f"x_raw{i}") for i, (c, n0, n) in enumerate(X_CHUNKS)]
-        x_grp = [
-            keep.tile([P, n, PACK], BF16, align_bytes=64, name=f"x_grp{i}", tag=("xg0", "xg1", "turn")[i])
-            for i, (c, n0, n) in enumerate(X_CHUNKS)
+        w1_raw = [[keep.tile([P, PACK, PACK * (m1 - m0)], F32, name=f"w1_raw{i}_{c}") for c in range(PASSES)] for i, (m0, m1) in enumerate(W1_GROUPS)]
+        w1_grp = keep.tile([P, PASSES, 264, PACK], BF16, align_bytes=64, name="w1_grp")
+        zero_a = keep.tile([P, 1], F32, align_bytes=64, name="zero_a", tag="grp2")
+        zero_b = keep.tile([P, 1], F32, align_bytes=64, name="zero_b", tag="grp3")
+        zero_c = keep.tile([P, 1], F32, align_bytes=64, name="zero_c", tag="w2_grp")
+        for zero in (zero_a, zero_b, zero_c):
+            nc.gpsimd.memset(zero[:], 0.0)
+        w1_codes = [
+            keep.tile([P, PASSES, P], U32, align_bytes=64, name=f"w1_codes{t}") if t != 2 else None for t in range(TILES)
         ]
-        w1_grp = {}
+        w1_scales = [keep.tile([P, PASSES, P], U8, align_bytes=64, name=f"w1_scales{t}") for t in range(TILES)]
+        x_raw = [keep.tile([P, PACK, T], F32, name=f"x_raw{c}") for c in range(PASSES)]
+        x_grp = [keep.tile([P, T, PACK], BF16, align_bytes=64, name=f"x_grp{c}") for c in range(PASSES)]
         x_codes = keep.tile([P, PASSES, T], U32, align_bytes=64, name="x_codes")
         x_scales = keep.tile([P, PASSES, T], U8, align_bytes=64, name="x_scales")
         w2_raw = keep.tile([P, PACK, N], F32, name="w2_raw")
-        w2_grp = keep.tile([P, N, PACK], BF16, align_bytes=64, name="w2_grp")
         w2_codes = keep.tile([P, N], U32, align_bytes=64, name="w2_codes")
         w2_scales = keep.tile([P, N], U8, align_bytes=64, name="w2_scales")
         gate_sb = [keep.tile([P, 2, V], F32, name=f"gate{d}") for d in range(2)]
@@ -69,13 +73,12 @@ def tile_picked_gcn_mlp_gelu_sub_l_kernel(
         w1r = w1.rearrange("(c p j) i -> c p j i", p=P, j=PACK)
 
         def load_w1(i):
-            i0, n = W1_BLOCKS[i]
+            m0, m1 = W1_GROUPS[i]
             for c in range(PASSES):
-                nc.sync.dma_start(out=w1_raw[i][c][:], in_=w1r[c, :, :, i0 : i0 + n])
+                nc.sync.dma_start(out=w1_raw[i][c][:], in_=w1r[c, :, :, PACK * m0 : PACK * m1])
 
-        def load_x(i):
-            c, n0, n = X_CHUNKS[i]
-            nc.sync.dma_start(out=x_raw[i][:], in_=xr[c, :, :, n0 : n0 + n])
+        def load_x(c):
+            nc.sync.dma_start(out=x_raw[c][:], in_=xr[c])
 
         def load_list(d):
             nc.sync.dma_start(lists[d][:], (pos1, pos2, pos3, pos4)[d])
@@ -85,7 +88,6 @@ def tile_picked_gcn_mlp_gelu_sub_l_kernel(
         load_x(1)
         for d in range(D):
             load_list(d)
-        load_x(2)
         load_w1(1)
         nc.sync.dma_start(out=gate_sb[0][:], in_=gate[0:2].rearrange("d p v -> p d v"))
         nc.sync.dma_start(out=gate_sb[1][:], in_=gate[2:4].rearrange("d p v -> p d v"))
@@ -96,25 +98,40 @@ def tile_picked_gcn_mlp_gelu_sub_l_kernel(
         nc.scalar.activation(warm[:], warm[:], GELU)
         make_identity(nc, ident[:])
 
-        def regroup_w1(engine_copy, t, c):
-            if c == 0:
-                w1_grp[t] = keep.tile(
-                    [P, PASSES, P, PACK], BF16, align_bytes=64, name=f"w1_grp{t}", tag=("wg0", "turn", "turn", "wg3")[t]
-                )
-            if t < 2:
-                interleave(engine_copy, w1_grp[t][:, c], w1_raw[t][c][:])
-            else:
+        def regroup_w1(engine_copy, i, c):
+            m0, m1 = W1_GROUPS[i]
+            src = w1_raw[i][c][:].rearrange("p j (m s) -> p m j s", s=PACK)
+            if i < 2:
                 engine_copy(
-                    out=w1_grp[t][:, c].rearrange("p (m r) j -> p m j r", r=2),
-                    in_=w1_raw[2][c][:].rearrange("p j (m h r) -> p h m j r", h=2, r=2)[:, t - 2],
+                    out=w1_grp[:, c, LANES * m0 : LANES * m1, :].rearrange("p (m r) j -> p m j r", r=LANES),
+                    in_=src[:, :, :, 0:LANES],
+                )
+            else:
+                engine_copy(out=w1_grp_2[:, c, 0:2, :].rearrange("p r j -> p j r"), in_=src[:, 0, :, 1:LANES])
+                engine_copy(
+                    out=w1_grp_2[:, c, 2:P, :].rearrange("p (m r) j -> p m j r", r=LANES),
+                    in_=src[:, 1:, :, 0:LANES],
                 )
 
-        def quantize_w1(t):
-            nc.vector.quantize_mx(
-                out=w1_codes[t][:].rearrange("p c n -> p (c n)").bitcast(FP8X4),
-                scales=w1_scales[t][:].rearrange("p c n -> p (c n)"),
-                in_=w1_grp[t][:].rearrange("p c n j -> p (c n j)"),
+        def regroup_last(engine_copy, i, c):
+            m0, m1 = W1_GROUPS[i]
+            skip = 1 if i == 2 else 0
+            engine_copy(
+                out=w1_grp_last[:, c, m0 + skip : m1, :],
+                in_=w1_raw[i][c][:].rearrange("p j (m s) -> p m j s", s=PACK)[:, skip:, :, LANES],
             )
+
+        def quantize_w1(t):
+            if t < 2:
+                for c in range(PASSES):
+                    quantize(nc, w1_codes[t][:, c], w1_scales[t][:, c], w1_grp[:, c, t * P : (t + 1) * P, :])
+            else:
+                grp = w1_grp_2 if t == 2 else w1_grp_last
+                nc.vector.quantize_mx(
+                    out=w1_codes[t][:].rearrange("p c n -> p (c n)").bitcast(FP8X4),
+                    scales=w1_scales[t][:].rearrange("p c n -> p (c n)"),
+                    in_=grp[:].rearrange("p c n j -> p (c n j)"),
+                )
 
         h_sb = [keep.tile([P, T], F32, name=f"h{t}") for t in range(TILES)]
 
@@ -132,112 +149,125 @@ def tile_picked_gcn_mlp_gelu_sub_l_kernel(
                         stop=(c == PASSES - 1),
                     )
             for n0, n in spans:
-                nc.scalar.activation(h_sb[t][:, n0 : n0 + n], bank[:, n0 : n0 + n], GELU)
+                if t == 1:
+                    nc.scalar.activation(h_sb[t][:, n0 : n0 + n], bank[:, n0 : n0 + n], GELU, bias=(zero_a, zero_b)[n0 // 256][:])
+                elif t == 3:
+                    nc.scalar.activation(h_sb[t][:, n0 : n0 + n], bank[:, n0 : n0 + n], GELU, bias=zero_c[:])
+                else:
+                    nc.scalar.activation(h_sb[t][:, n0 : n0 + n], bank[:, n0 : n0 + n], GELU)
 
-        def quantize_x(i, a, n):
-            c, n0, m = X_CHUNKS[i]
-            quantize(nc, x_codes[:, c, n0 + a : n0 + a + n], x_scales[:, c, n0 + a : n0 + a + n], x_grp[i][:, a : a + n, :])
+        def regroup_x(engine_copy, c, n0, n):
+            interleave(engine_copy, x_grp[c][:, n0 : n0 + n, :], x_raw[c][:, :, n0 : n0 + n])
+
+        def quantize_x(c, n0, n):
+            quantize(nc, x_codes[:, c, n0 : n0 + n], x_scales[:, c, n0 : n0 + n], x_grp[c][:, n0 : n0 + n, :])
 
         regroup_w1(nc.vector.tensor_copy, 0, 0)
         regroup_w1(nc.scalar.copy, 0, 1)
         quantize_w1(0)
-        interleave(nc.vector.tensor_copy, x_grp[0][:, 0:256, :], x_raw[0][:, :, 0:256])
-        interleave(nc.scalar.copy, x_grp[0][:, 256:512, :], x_raw[0][:, :, 256:512])
+        regroup_x(nc.vector.tensor_copy, 0, 0, 256)
+        regroup_x(nc.scalar.copy, 0, 256, 256)
         quantize_x(0, 0, 256)
         quantize_x(0, 256, 256)
-        interleave(nc.vector.tensor_copy, x_grp[1][:, 0:256, :], x_raw[1][:, :, 0:256])
-        interleave(nc.scalar.copy, x_grp[1][:, 256:384, :], x_raw[1][:, :, 256:384])
-        quantize_x(1, 0, 256)
-        interleave(nc.vector.tensor_copy, x_grp[2][:], x_raw[2][:])
-        quantize_x(1, 256, 128)
-        quantize_x(2, 0, 128)
+        regroup_x(nc.vector.tensor_copy, 1, 0, 128)
+        regroup_x(nc.vector.tensor_copy, 1, 128, 128)
+        regroup_x(nc.scalar.copy, 1, 256, 128)
+        regroup_x(nc.scalar.copy, 1, 384, 128)
+        for n0 in (0, 128, 256, 384):
+            quantize_x(1, n0, 128)
         regroup_w1(nc.vector.tensor_copy, 1, 0)
         regroup_w1(nc.vector.tensor_copy, 1, 1)
         quantize_w1(1)
         project(0, ((0, 256), (256, 128), (384, 128)))
-        project(1, ((0, 512),))
+        project(1, ((0, 256), (256, 256)))
+        w1_grp_2 = keep.tile([P, PASSES, P, PACK], BF16, align_bytes=64, name="w1_grp_2", tag="grp2")
+        w1_grp_last = keep.tile([P, PASSES, P, PACK], BF16, align_bytes=64, name="w1_grp_last", tag="grp3")
 
-        z_bank = [psum.tile([P, H], F32, name=f"z_bank{b}") for b in range(BLOCKS)]
-        z_rows = [keep.tile([P, PACK, P], F32, name=f"z_rows{b}") for b in range(BLOCKS)]
+        z_bank = [psum.tile([P, LANES * P], F32, name=f"z_bank{b}") for b in range(BLOCKS)]
+        z_rows = [keep.tile([P, LANES, P], F32, name=f"z_rows{b}") for b in range(BLOCKS)]
+        z_grp = [keep.tile([P, P, PACK], BF16, align_bytes=64, name=f"z_grp{b}") for b in range(BLOCKS)]
+        z_codes = [keep.tile([P, P], U32, align_bytes=64, name=f"z_codes{b}") for b in range(BLOCKS)]
+        z_scales = [keep.tile([P, P], U8, align_bytes=64, name=f"z_scales{b}") for b in range(BLOCKS)]
+        pair = keep.tile([P, 2, V], F32, name="pair")
+        rest = keep.tile([P, 2, V], F32, name="rest")
+        nc.gpsimd.memset(rest[:, 0, :], 0.0)
 
-        def gather(t, d, v0, n):
-            g = keep.tile([P, n], F32, name=f"g{t}_{d}_{v0}")
+        def gather(t, d, v0, n, into=None):
+            if into is None:
+                into_tile = keep.tile([P, n], F32, align_bytes=64, name=f"g{t}_{d}_{v0}", tag=f"g{t}_{d}")
+                into = into_tile[:]
             nc.vector.tensor_tensor(
-                g[:], h_sb[t][:].indirect(lists[d][:, v0 // 16 : (v0 + n) // 16]), gate_sb[d // 2][:, d % 2, v0 : v0 + n], MULT
+                into, h_sb[t][:].indirect(lists[d][:, v0 // 16 : (v0 + n) // 16]), gate_sb[d // 2][:, d % 2, v0 : v0 + n], MULT
             )
-            return g
+            return into
 
-        def add_tile(t, parts):
+        def add_part(t, d):
+            part = gather(t, d, 0, V)
             for b in range(BLOCKS):
-                add_up(t, b, [g[:, b * P : (b + 1) * P] for g in parts])
-
-        def add_up(t, b, parts):
-            for d in range(D):
                 nc.tensor.matmul(
                     z_bank[b][:, t * P : (t + 1) * P],
-                    lhsT=parts[d],
+                    lhsT=part[:, b * P : (b + 1) * P],
                     rhs=ident[:],
                     is_transpose=True,
                     start=(d == 0),
                     stop=(d == D - 1),
                 )
 
-        def sort_rows(copy, b, t):
-            if t < 2:
-                rows = z_rows[b][:, :, t * 32 : (t + 1) * 32]
-                cols = z_bank[b][:, t * P : (t + 1) * P].rearrange("v (m s) -> v s m", s=PACK)
-            else:
-                rows = z_rows[b][:, 2 * t - 4 : 2 * t - 2, 64:128]
-                cols = z_bank[b][:, t * P : (t + 1) * P].rearrange("v (m r) -> v r m", r=2)
-            copy(rows, cols)
+        def sort_rows(b, m0, m1):
+            nc.scalar.copy(
+                z_rows[b][:, :, m0:m1], z_bank[b][:, LANES * m0 : LANES * m1].rearrange("v (m s) -> v s m", s=LANES)
+            )
 
+        for d in range(D):
+            add_part(0, d)
+
+        for c in range(PASSES):
+            regroup_last(nc.scalar.copy, 0, c)
         for c in range(PASSES):
             regroup_w1(nc.scalar.copy, 2, c)
-        parts = [gather(0, d, 0, V) for d in range(D)]
-        add_tile(0, parts)
-
-        parts = [gather(1, 0, 0, V)]
+        add_part(1, 0)
+        add_part(1, 1)
+        w1_codes[2] = keep.tile([P, PASSES, P], U32, align_bytes=64, name="w1_codes2", tag="g1_0")
         quantize_w1(2)
         project(2, ((0, 512),))
-        for c in range(PASSES):
-            regroup_w1(nc.scalar.copy, 3, c)
-        parts += [gather(1, d, 0, V) for d in (1, 2)]
+        for i in (1, 2):
+            for c in range(PASSES):
+                regroup_last(nc.scalar.copy, i, c)
+        add_part(1, 2)
+        add_part(1, 3)
         quantize_w1(3)
         project(3, ((0, 512),))
-        parts += [gather(1, 3, 0, V)]
-        add_tile(1, parts)
+        for b in range(BLOCKS):
+            sort_rows(b, 0, 85)
 
+        w2_grp = keep.tile([P, N, PACK], BF16, align_bytes=64, name="w2_grp", tag="w2_grp")
         interleave(nc.scalar.copy, w2_grp[:], w2_raw[:])
-        parts = [gather(2, d, 0, V) for d in range(D)]
-        add_tile(2, parts)
-        z_grp = [keep.tile([P, P, PACK], BF16, align_bytes=64, name=f"z_grp{b}") for b in range(BLOCKS)]
-        z_codes = [keep.tile([P, P], U32, align_bytes=64, name=f"z_codes{b}") for b in range(BLOCKS)]
-        z_scales = [keep.tile([P, P], U8, align_bytes=64, name=f"z_scales{b}") for b in range(BLOCKS)]
-        empty = (nc.scalar.copy, nc.vector.tensor_copy)
-
-        def turn_back(b, u):
-            back = psum.tile([P, 2, P], F32, name=f"back{b}")
-            for r in range(2):
-                nc.tensor.transpose(back[:, r, :], z_rows[b][:, 2 * u + r, :], ident[:])
-            return back
-
-        def round_pair(copy, b, u, back):
-            copy(z_grp[b][:, :, 2 * u : 2 * u + 2], back[:].rearrange("p r v -> p v r"))
-
+        for d in range(D):
+            add_part(2, d)
         for b in range(BLOCKS):
-            for t in range(3):
-                sort_rows(nc.scalar.copy, b, t)
-            round_pair(nc.scalar.copy, b, 0, turn_back(b, 0))
+            sort_rows(b, 85, 128)
+        for b in range(BLOCKS):
+            back = psum.tile([P, LANES, P], F32, name=f"back{b}")
+            for s in range(LANES):
+                nc.tensor.transpose(back[:, s, :], z_rows[b][:, s, :], ident[:])
+            nc.scalar.copy(z_grp[b][:, :, 0:2], back[:, 0:2, :].rearrange("p s v -> p v s"))
+            nc.scalar.copy(pair[:, 0, b * P : (b + 1) * P], back[:, 2, :])
+
         parts = [gather(3, d, 0, V) for d in (0, 1, 2)]
-        last = [gather(3, 3, b * P, P) for b in range(BLOCKS)]
+        some = keep.tile([P, V], F32, name="some")
+        nc.vector.tensor_tensor(some[:], parts[0], parts[1], ADD)
+        gather(3, 3, 0, P, rest[:, 1, 0:P])
+        nc.vector.tensor_tensor(pair[:, 1, :], some[:], parts[2], ADD)
+        gather(3, 3, P, P, rest[:, 1, P:V])
+        for b in range(BLOCKS):
+            cols = slice(b * P, (b + 1) * P)
+            nc.vector.tensor_tensor(
+                z_grp[b][:, :, 2:4],
+                pair[:, :, cols].rearrange("p s v -> p v s"),
+                rest[:, :, cols].rearrange("p s v -> p v s"),
+                ADD,
+            )
         quantize(nc, w2_codes[:], w2_scales[:], w2_grp[:])
-        for b in range(BLOCKS):
-            add_up(3, b, [g[:, b * P : (b + 1) * P] for g in parts] + [last[b][:]])
-        for b in range(BLOCKS):
-            sort_rows(empty[b], b, 3)
-        back = [turn_back(b, 1) for b in range(BLOCKS)]
-        for b in range(BLOCKS):
-            round_pair(empty[b], b, 1, back[b])
         for b in range(BLOCKS):
             quantize(nc, z_codes[b][:], z_scales[b][:], z_grp[b][:])
         outr = out.rearrange("(a p) v -> p a v", p=P)

from contextlib import ExitStack

import concourse.mybir as mybir
from concourse.masks import make_identity

K, T, D, V, H, N = 1024, 512, 4, 256, 512, 256
FLOPS = 2 * K * T * H + 2 * H * N * V

F32 = mybir.dt.float32
BF16 = mybir.dt.bfloat16
U32 = mybir.dt.uint32
U16 = mybir.dt.uint16
U8 = mybir.dt.uint8
FP8X4 = mybir.dt.float8_e4m3fn_x4
MULT = mybir.AluOpType.mult
ADD = mybir.AluOpType.add
GELU = mybir.ActivationFunctionType.Gelu_apprx_tanh

P = 128
PACK = 4
PASSES = K // (P * PACK)
TILES = H // P
BLOCKS = V // P
LANES = PACK - 1
W1_GROUPS = ((0, 43), (43, 86), (85, 128))


def interleave(engine_copy, dst, src):
    engine_copy(
        out=dst.rearrange("p (c i) j -> p c j i", i=4),
        in_=src.rearrange("p j (c i) -> p c j i", i=4),
    )


def quantize(nc, codes, scales, grouped):
    nc.vector.quantize_mx(
        out=codes.bitcast(FP8X4), scales=scales, in_=grouped.rearrange("p c j -> p (c j)")
    )


def tile_picked_gcn_mlp_gelu_sub_l_kernel(
    tc, xT, w1, w2, gate, pos1, pos2, pos3, pos4, out
):
    nc = tc.nc
    with ExitStack() as ctx:
        keep = ctx.enter_context(tc.tile_pool(name="keep", bufs=1))
        psum = ctx.enter_context(tc.psum_pool(name="psum", bufs=1))

        w1_raw = [[keep.tile([P, PACK, PACK * (m1 - m0)], F32, name=f"w1_raw{i}_{c}") for c in range(PASSES)] for i, (m0, m1) in enumerate(W1_GROUPS)]
        w1_grp = keep.tile([P, PASSES, 264, PACK], BF16, align_bytes=64, name="w1_grp")
        zero_a = keep.tile([P, 1], F32, align_bytes=64, name="zero_a", tag="grp2")
        zero_b = keep.tile([P, 1], F32, align_bytes=64, name="zero_b", tag="grp3")
        zero_c = keep.tile([P, 1], F32, align_bytes=64, name="zero_c", tag="w2_grp")
        for zero in (zero_a, zero_b, zero_c):
            nc.gpsimd.memset(zero[:], 0.0)
        w1_codes = [
            keep.tile([P, PASSES, P], U32, align_bytes=64, name=f"w1_codes{t}") if t != 2 else None for t in range(TILES)
        ]
        w1_scales = [keep.tile([P, PASSES, P], U8, align_bytes=64, name=f"w1_scales{t}") for t in range(TILES)]
        x_raw = [keep.tile([P, PACK, T], F32, name=f"x_raw{c}") for c in range(PASSES)]
        x_grp = [keep.tile([P, T, PACK], BF16, align_bytes=64, name=f"x_grp{c}") for c in range(PASSES)]
        x_codes = keep.tile([P, PASSES, T], U32, align_bytes=64, name="x_codes")
        x_scales = keep.tile([P, PASSES, T], U8, align_bytes=64, name="x_scales")
        w2_raw = keep.tile([P, PACK, N], F32, name="w2_raw")
        w2_codes = keep.tile([P, N], U32, align_bytes=64, name="w2_codes")
        w2_scales = keep.tile([P, N], U8, align_bytes=64, name="w2_scales")
        gate_sb = [keep.tile([P, 2, V], F32, name=f"gate{d}") for d in range(2)]
        lists = [keep.tile([P, V // 16], U16, name=f"list{d}") for d in range(D)]
        ident = keep.tile([P, P], F32, name="ident")
        warm = keep.tile([P, 1], F32, name="warm")

        xr = xT.rearrange("(c p j) t -> c p j t", p=P, j=PACK)
        w1r = w1.rearrange("(c p j) i -> c p j i", p=P, j=PACK)

        def load_w1(i):
            m0, m1 = W1_GROUPS[i]
            for c in range(PASSES):
                nc.sync.dma_start(out=w1_raw[i][c][:], in_=w1r[c, :, :, PACK * m0 : PACK * m1])

        def load_x(c):
            nc.sync.dma_start(out=x_raw[c][:], in_=xr[c])

        def load_list(d):
            nc.sync.dma_start(lists[d][:], (pos1, pos2, pos3, pos4)[d])

        load_w1(0)
        load_x(0)
        load_x(1)
        for d in range(D):
            load_list(d)
        load_w1(1)
        nc.sync.dma_start(out=gate_sb[0][:], in_=gate[0:2].rearrange("d p v -> p d v"))
        nc.sync.dma_start(out=gate_sb[1][:], in_=gate[2:4].rearrange("d p v -> p d v"))
        load_w1(2)
        nc.sync.dma_start(out=w2_raw[:], in_=w2.rearrange("(p j) m -> p j m", j=PACK))

        nc.gpsimd.memset(warm[:], 0.0)
        nc.scalar.activation(warm[:], warm[:], GELU)
        make_identity(nc, ident[:])

        def regroup_w1(engine_copy, i, c):
            m0, m1 = W1_GROUPS[i]
            src = w1_raw[i][c][:].rearrange("p j (m s) -> p m j s", s=PACK)
            if i < 2:
                engine_copy(
                    out=w1_grp[:, c, LANES * m0 : LANES * m1, :].rearrange("p (m r) j -> p m j r", r=LANES),
                    in_=src[:, :, :, 0:LANES],
                )
            else:
                engine_copy(out=w1_grp_2[:, c, 0:2, :].rearrange("p r j -> p j r"), in_=src[:, 0, :, 1:LANES])
                engine_copy(
                    out=w1_grp_2[:, c, 2:P, :].rearrange("p (m r) j -> p m j r", r=LANES),
                    in_=src[:, 1:, :, 0:LANES],
                )

        def regroup_last(engine_copy, i, c):
            m0, m1 = W1_GROUPS[i]
            skip = 1 if i == 2 else 0
            engine_copy(
                out=w1_grp_last[:, c, m0 + skip : m1, :],
                in_=w1_raw[i][c][:].rearrange("p j (m s) -> p m j s", s=PACK)[:, skip:, :, LANES],
            )

        def quantize_w1(t):
            if t < 2:
                for c in range(PASSES):
                    quantize(nc, w1_codes[t][:, c], w1_scales[t][:, c], w1_grp[:, c, t * P : (t + 1) * P, :])
            else:
                grp = w1_grp_2 if t == 2 else w1_grp_last
                nc.vector.quantize_mx(
                    out=w1_codes[t][:].rearrange("p c n -> p (c n)").bitcast(FP8X4),
                    scales=w1_scales[t][:].rearrange("p c n -> p (c n)"),
                    in_=grp[:].rearrange("p c n j -> p (c n j)"),
                )

        h_sb = [keep.tile([P, T], F32, name=f"h{t}") for t in range(TILES)]

        def project(t, spans):
            bank = psum.tile([P, T], F32, name=f"h_bank{t % 3}")
            for n0, n in spans:
                for c in range(PASSES):
                    nc.tensor.matmul_mx(
                        out=bank[:, n0 : n0 + n],
                        lhsT=w1_codes[t][:, c, :].bitcast(FP8X4),
                        lhsT_scale=w1_scales[t][:, c, :],
                        rhs=x_codes[:, c, n0 : n0 + n].bitcast(FP8X4),
                        rhs_scale=x_scales[:, c, n0 : n0 + n],
                        start=(c == 0),
                        stop=(c == PASSES - 1),
                    )
            for n0, n in spans:
                if t == 1:
                    nc.scalar.activation(h_sb[t][:, n0 : n0 + n], bank[:, n0 : n0 + n], GELU, bias=(zero_a, zero_b)[n0 // 256][:])
                elif t == 3:
                    nc.scalar.activation(h_sb[t][:, n0 : n0 + n], bank[:, n0 : n0 + n], GELU, bias=zero_c[:])
                else:
                    nc.scalar.activation(h_sb[t][:, n0 : n0 + n], bank[:, n0 : n0 + n], GELU)

        def regroup_x(engine_copy, c, n0, n):
            interleave(engine_copy, x_grp[c][:, n0 : n0 + n, :], x_raw[c][:, :, n0 : n0 + n])

        def quantize_x(c, n0, n):
            quantize(nc, x_codes[:, c, n0 : n0 + n], x_scales[:, c, n0 : n0 + n], x_grp[c][:, n0 : n0 + n, :])

        regroup_w1(nc.vector.tensor_copy, 0, 0)
        regroup_w1(nc.scalar.copy, 0, 1)
        quantize_w1(0)
        regroup_x(nc.vector.tensor_copy, 0, 0, 256)
        regroup_x(nc.scalar.copy, 0, 256, 256)
        quantize_x(0, 0, 256)
        quantize_x(0, 256, 256)
        regroup_x(nc.vector.tensor_copy, 1, 0, 128)
        regroup_x(nc.vector.tensor_copy, 1, 128, 128)
        regroup_x(nc.scalar.copy, 1, 256, 128)
        regroup_x(nc.scalar.copy, 1, 384, 128)
        for n0 in (0, 128, 256, 384):
            quantize_x(1, n0, 128)
        regroup_w1(nc.vector.tensor_copy, 1, 0)
        regroup_w1(nc.vector.tensor_copy, 1, 1)
        quantize_w1(1)
        project(0, ((0, 256), (256, 128), (384, 128)))
        project(1, ((0, 256), (256, 256)))
        w1_grp_2 = keep.tile([P, PASSES, P, PACK], BF16, align_bytes=64, name="w1_grp_2", tag="grp2")
        w1_grp_last = keep.tile([P, PASSES, P, PACK], BF16, align_bytes=64, name="w1_grp_last", tag="grp3")

        z_bank = [psum.tile([P, LANES * P], F32, name=f"z_bank{b}") for b in range(BLOCKS)]
        z_rows = [keep.tile([P, LANES, P], F32, name=f"z_rows{b}") for b in range(BLOCKS)]
        z_grp = [keep.tile([P, P, PACK], BF16, align_bytes=64, name=f"z_grp{b}") for b in range(BLOCKS)]
        z_codes = [keep.tile([P, P], U32, align_bytes=64, name=f"z_codes{b}") for b in range(BLOCKS)]
        z_scales = [keep.tile([P, P], U8, align_bytes=64, name=f"z_scales{b}") for b in range(BLOCKS)]
        pair = keep.tile([P, 2, V], F32, name="pair")
        rest = keep.tile([P, 2, V], F32, name="rest")
        nc.gpsimd.memset(rest[:, 0, :], 0.0)

        def gather(t, d, v0, n, into=None):
            if into is None:
                into_tile = keep.tile([P, n], F32, align_bytes=64, name=f"g{t}_{d}_{v0}", tag=f"g{t}_{d}")
                into = into_tile[:]
            nc.vector.tensor_tensor(
                into, h_sb[t][:].indirect(lists[d][:, v0 // 16 : (v0 + n) // 16]), gate_sb[d // 2][:, d % 2, v0 : v0 + n], MULT
            )
            return into

        def add_part(t, d):
            part = gather(t, d, 0, V)
            for b in range(BLOCKS):
                nc.tensor.matmul(
                    z_bank[b][:, t * P : (t + 1) * P],
                    lhsT=part[:, b * P : (b + 1) * P],
                    rhs=ident[:],
                    is_transpose=True,
                    start=(d == 0),
                    stop=(d == D - 1),
                )

        def sort_rows(b, m0, m1):
            nc.scalar.copy(
                z_rows[b][:, :, m0:m1], z_bank[b][:, LANES * m0 : LANES * m1].rearrange("v (m s) -> v s m", s=LANES)
            )

        for d in range(D):
            add_part(0, d)

        for c in range(PASSES):
            regroup_last(nc.scalar.copy, 0, c)
        for c in range(PASSES):
            regroup_w1(nc.scalar.copy, 2, c)
        add_part(1, 0)
        add_part(1, 1)
        w1_codes[2] = keep.tile([P, PASSES, P], U32, align_bytes=64, name="w1_codes2", tag="g1_0")
        quantize_w1(2)
        project(2, ((0, 512),))
        for i in (1, 2):
            for c in range(PASSES):
                regroup_last(nc.scalar.copy, i, c)
        add_part(1, 2)
        add_part(1, 3)
        quantize_w1(3)
        project(3, ((0, 512),))
        for b in range(BLOCKS):
            sort_rows(b, 0, 85)

        w2_grp = keep.tile([P, N, PACK], BF16, align_bytes=64, name="w2_grp", tag="w2_grp")
        interleave(nc.scalar.copy, w2_grp[:], w2_raw[:])
        for d in range(D):
            add_part(2, d)
        for b in range(BLOCKS):
            sort_rows(b, 85, 128)
        for b in range(BLOCKS):
            back = psum.tile([P, LANES, P], F32, name=f"back{b}")
            for s in range(LANES):
                nc.tensor.transpose(back[:, s, :], z_rows[b][:, s, :], ident[:])
            nc.scalar.copy(z_grp[b][:, :, 0:2], back[:, 0:2, :].rearrange("p s v -> p v s"))
            nc.scalar.copy(pair[:, 0, b * P : (b + 1) * P], back[:, 2, :])

        parts = [gather(3, d, 0, V) for d in (0, 1, 2)]
        some = keep.tile([P, V], F32, name="some")
        nc.vector.tensor_tensor(some[:], parts[0], parts[1], ADD)
        gather(3, 3, 0, P, rest[:, 1, 0:P])
        nc.vector.tensor_tensor(pair[:, 1, :], some[:], parts[2], ADD)
        gather(3, 3, P, P, rest[:, 1, P:V])
        for b in range(BLOCKS):
            cols = slice(b * P, (b + 1) * P)
            nc.vector.tensor_tensor(
                z_grp[b][:, :, 2:4],
                pair[:, :, cols].rearrange("p s v -> p v s"),
                rest[:, :, cols].rearrange("p s v -> p v s"),
                ADD,
            )
        quantize(nc, w2_codes[:], w2_scales[:], w2_grp[:])
        for b in range(BLOCKS):
            quantize(nc, z_codes[b][:], z_scales[b][:], z_grp[b][:])
        outr = out.rearrange("(a p) v -> p a v", p=P)

        def second(bank, b, a):
            nc.tensor.matmul_mx(
                out=bank,
                lhsT=w2_codes[:, a * P : (a + 1) * P].bitcast(FP8X4),
                lhsT_scale=w2_scales[:, a * P : (a + 1) * P],
                rhs=z_codes[b][:].bitcast(FP8X4),
                rhs_scale=z_scales[b][:],
                start=True,
                stop=True,
            )

        o_bank0 = psum.tile([P, T], F32, name="h_bank1")
        o_sb0 = keep.tile([P, 2, P], F32, name="o_sb0")
        for a in range(2):
            second(o_bank0[:, a * P : (a + 1) * P], 0, a)
        nc.scalar.copy(o_sb0[:], o_bank0[:, 0:256].rearrange("p (a v) -> p a v", a=2))
        nc.sync.dma_start(out=outr[:, :, 0:P], in_=o_sb0[:])
        for a, copy, store in ((0, nc.vector.tensor_copy, nc.sync.dma_start), (1, nc.scalar.copy, nc.scalar.dma_start)):
            o_bank1 = psum.tile([P, T], F32, name=("h_bank2", "o_bank")[a])
            o_sb1 = keep.tile([P, P], F32, name=f"o_sb1_{a}")
            second(o_bank1[:, 0:P], 1, a)
            copy(o_sb1[:], o_bank1[:, 0:P])
            store(out=outr[:, a, P:V], in_=o_sb1[:])
